import numpy as np
import ml_dtypes


def mxq(x, axis, fmt="e4m3"):
    dtype, down = {"e4m3": (ml_dtypes.float8_e4m3fn, 7), "e5m2": (ml_dtypes.float8_e5m2, 14)}[fmt]
    v = np.moveaxis(np.asarray(x, np.float32).astype(ml_dtypes.bfloat16).astype(np.float64), axis, -1)
    blocks = v.reshape(v.shape[:-1] + (-1, 32))
    amax = np.abs(blocks).max(-1, keepdims=True)
    byte = np.maximum(np.where(amax > 0, np.frexp(amax)[1] - 1 + 127, 0) - down, 1)
    scale = np.exp2(byte - 127.0)
    codes = (blocks / scale).astype(np.float32).astype(dtype).astype(np.float64)
    return np.moveaxis((codes * scale).reshape(v.shape), -1, axis)


WIDE = False


def mx_kscale(k):
    if not WIDE:
        return np.ones(k)
    levels = np.array([10, -10, 5, -5, 0])
    if k % 512:
        return np.exp2(np.random.permutation(np.resize(levels, k // 32))).repeat(32)
    a = np.empty((k // 512, 16))
    for p in range(k // 512):
        a[p, :8] = np.random.permutation(np.resize(levels, 8))
        for g in range(8):
            far = levels[np.abs(levels - a[p, g]) >= 10]
            a[p, g + 8] = far[np.random.randint(len(far))]
    return np.exp2(a.ravel()).repeat(32)


def f64(x):
    return np.asarray(x).astype(np.float64)


def striped(idx):
    return np.tile(idx.reshape(-1, 16).T, (8, 1)).astype(np.uint16)


def unstriped(offs):
    return offs[:16].T.reshape(-1).astype(np.int64)


E2M1 = np.array([0.0, 0.5, 1.0, 1.5, 2.0, 3.0, 4.0, 6.0, -0.0, -0.5, -1.0, -1.5, -2.0, -3.0, -4.0, -6.0])


def pack_weight(w, fmt):
    k, n = w.shape
    w = f64(np.asarray(w, np.float32).astype(ml_dtypes.bfloat16)).reshape(k // 32, 32, n)
    amax = np.abs(w).max(1)
    if fmt == "e4m3":
        byte = np.frexp(amax)[1] - 1 + 127 - 7
    else:
        mant, ex = np.frexp(amax / 6.0)
        byte = np.where(mant > 0.5, ex, ex - 1) + 127
    byte = np.clip(np.where(amax > 0, byte, 1), 1, 254)
    scaled = (w * np.exp2(127.0 - byte)[:, None, :]).reshape(k, n).astype(np.float32)
    by_word = np.ascontiguousarray(scaled.reshape(k // 512, 128, 4, n).transpose(0, 1, 3, 2))
    if fmt == "e4m3":
        words = by_word.astype(ml_dtypes.float8_e4m3fn).view(np.uint8)
    else:
        c = by_word.astype(ml_dtypes.float4_e2m1fn).view(np.uint8) & 0xF
        words = (c[..., 0::2] | (c[..., 1::2] << 4)).reshape(k // 512, 128, 2 * n)
    return np.ascontiguousarray(words), np.ascontiguousarray(byte.astype(np.uint8).reshape(k // 512, 16, n))


def unpack_weight(words, scales, fmt):
    g, _, n = scales.shape
    words = np.ascontiguousarray(words).reshape(g, 128, n, -1)
    if fmt == "e4m3":
        vals = words.view(ml_dtypes.float8_e4m3fn).astype(np.float64)
    else:
        nib = np.empty((g, 128, n, 4), np.uint8)
        nib[..., 0::2] = words & 0xF
        nib[..., 1::2] = words >> 4
        vals = E2M1[nib]
    vals = vals * np.repeat(np.exp2(scales.astype(np.float64) - 127.0), 8, axis=1)[..., None]
    return vals.transpose(0, 1, 3, 2).reshape(g * 512, n)


def pack_table(v):
    words, scales = pack_weight(v, "e4m3")
    return np.concatenate([words.reshape(words.shape[0], -1), scales.reshape(scales.shape[0], -1)], axis=1)


def unpack_table(tab):
    g, t = tab.shape[0], tab.shape[1] // 528
    return unpack_weight(tab[:, :512 * t].reshape(g, 128, t, 4), tab[:, 512 * t:].reshape(g, 16, t), "e4m3")


O, K, M, T, S = 1024, 1536, 512, 4096, 2048


def setup_inputs():
    n = np.random.standard_normal
    s = mx_kscale(K)[:, None]
    w = n((K, M)) / np.sqrt(K) / s
    p_w4 = pack_weight(w[O:], "e2m1")
    return {
        "tab": pack_table(n((K, T)) * s),
        "w8": (w[:O]).astype(np.float32),
        "w4_words": p_w4[0],
        "w4_scales": p_w4[1],
        "gate": (n((512, 2048))).astype(np.float32),
        "offs": striped(np.random.permutation(T)[:S]),
    }


def reference(tab, w8, w4_words, w4_scales, gate, offs):
    tab_ = unpack_table(tab)[:, unstriped(offs)]
    w8_ = mxq(f64(w8), 0, "e4m3")
    w4_ = unpack_weight(w4_words, w4_scales, "e2m1")
    y = w8_.T @ tab_[:O] + w4_.T @ tab_[O:]
    return f64(gate) * y

@@ -1,0 +1,129 @@
+from contextlib import ExitStack
+
+import concourse.mybir as mybir
+
+O, K, N, T, S = 1024, 1536, 512, 4096, 2048
+FLOPS = 2 * N * S * K
+
+P = 128
+PACK = 4
+K_PASS = P * PACK
+PASSES = K // K_PASS
+W8_PASSES = O // K_PASS
+M_TILES = N // P
+BANK = 512
+PAIR = 2 * BANK
+ROWS = 4
+
+F32 = mybir.dt.float32
+BF16 = mybir.dt.bfloat16
+I32 = mybir.dt.int32
+U32 = mybir.dt.uint32
+U16 = mybir.dt.uint16
+U8 = mybir.dt.uint8
+E4M3 = mybir.dt.float8_e4m3fn_x4
+E2M1 = mybir.dt.float4_e2m1fn_x4
+MULT = mybir.AluOpType.mult
+COPY = mybir.ActivationFunctionType.Copy
+
+PLANE = (4, 8, 0)
+
+
+def tile_list_tabo_mul_kernel(tc, tab, w8, w4_words, w4_scales, gate, offs, out):
+    nc = tc.nc
+    with ExitStack() as ctx:
+        keep = ctx.enter_context(tc.tile_pool(name="keep", bufs=1))
+        psum = ctx.enter_context(tc.psum_pool(name="psum", bufs=1))
+
+        offsets = keep.tile([P, S // 16], U16, name="offsets")
+        words = [keep.tile([P, T], I32, align_bytes=64, name=f"words{a}") for a in range(PASSES)]
+        planes = keep.tile([P, T // 4], I32, align_bytes=64, name="planes")
+        w4_plane = keep.tile([P, N // 4], I32, align_bytes=64, name="w4_plane")
+        w4_codes = keep.tile([P, 2 * N], U8, align_bytes=64, name="w4_codes")
+        w_raw = [keep.tile([P, PACK, N], F32, align_bytes=64, name=f"w_raw{a}") for a in range(W8_PASSES)]
+        w_grouped = [keep.tile([P, N, PACK], BF16, align_bytes=64, name=f"w_grouped{a}") for a in range(W8_PASSES)]
+        w_codes = [keep.tile([P, N], U32, align_bytes=64, name=f"w_codes{a}") for a in range(W8_PASSES)]
+        w_plane = [keep.tile([P, N], U8, align_bytes=64, name=f"w_plane{a}") for a in range(W8_PASSES)]
+        picked = [keep.tile([P, S], U32, align_bytes=64, name=f"picked{a}") for a in range(PASSES)]
+        picked_planes = keep.tile([P, S], U8, align_bytes=64, name="picked_planes")
+        gates = {}
+        results = {}
+        for h in range(S // PAIR):
+            for m in range(M_TILES):
+                gates[h, m] = keep.tile([P, PAIR], F32, align_bytes=64, name=f"gate{h}{m}")
+                results[h, m] = keep.tile([P, PAIR], F32, align_bytes=64, name=f"result{h}{m}")
+
+        def load_words(a):
+            nc.sync.dma_start(words[a][:], tab[a, 0 : 512 * T].rearrange("(p b) -> p b", p=P).bitcast(I32))
+
+        load_words(0)
+        nc.sync.dma_start(offsets[:], offs)
+        nc.vector.memset(planes[:], 0)
+        nc.vector.memset(w4_plane[:], 0)
+        for a in range(PASSES):
+            rows = tab[a, 512 * T : 528 * T].rearrange("(q t) -> q t", q=16).bitcast(I32)
+            for quadrant in range(4):
+                first = 32 * quadrant + PLANE[a]
+                nc.gpsimd.dma_start(planes[first : first + ROWS, :], rows[ROWS * quadrant : ROWS * (quadrant + 1), :])
+        for quadrant in range(4):
+            nc.gpsimd.dma_start(
+                w4_plane[32 * quadrant : 32 * quadrant + ROWS, :],
+                w4_scales[0, ROWS * quadrant : ROWS * (quadrant + 1), :].bitcast(I32),
+            )
+        for a in range(W8_PASSES):
+            nc.sync.dma_start(w_raw[a][:], w8[a * K_PASS : (a + 1) * K_PASS, :].rearrange("(p j) n -> p j n", j=PACK))
+        nc.sync.dma_start(w4_codes[:].bitcast(I32), w4_words[0].bitcast(I32))
+        for a in range(1, PASSES):
+            load_words(a)
+        for h in range(S // PAIR):
+            for m in range(M_TILES):
+                nc.sync.dma_start(gates[h, m][:], gate[m * P : (m + 1) * P, h * PAIR : (h + 1) * PAIR])
+
+        def gather_words(a, lo, hi):
+            nc.vector.tensor_copy(
+                picked[a][:, lo:hi], words[a][:].bitcast(U32).indirect(offsets[:, lo // 16 : hi // 16])
+            )
+
+        gather_words(0, 0, S)
+        nc.vector.tensor_copy(picked_planes[:], planes[:].bitcast(U8).indirect(offsets[:]))
+        for a in range(W8_PASSES):
+            nc.scalar.activation(w_grouped[a][:], w_raw[a][:].rearrange("p j n -> p n j"), COPY)
+            nc.vector.quantize_mx(
+                out=w_codes[a][:].bitcast(E4M3),
+                scales=w_plane[a][:],
+                in_=w_grouped[a][:].rearrange("p n j -> p (n j)"),
+            )
+        gather_words(1, 0, S)
+
+        def stationary(a, m):
+            cols = slice(m * P, (m + 1) * P)
+            if a < W8_PASSES:
+                return w_codes[a][:, cols].bitcast(E4M3), w_plane[a][:, cols]
+            return w4_codes[:, 2 * m * P : 2 * (m + 1) * P].bitcast(E2M1), w4_plane[:].bitcast(U8)[:, cols]
+
+        for h in range(S // PAIR):
+            for b in range(2):
+                gather_words(2, h * PAIR + b * BANK, h * PAIR + (b + 1) * BANK)
+            banks = {}
+            for m in range(M_TILES):
+                for b in range(2):
+                    banks[m, b] = psum.tile([P, BANK], F32, name=f"bank{m}{b}")
+            for a in range(PASSES):
+                for m in range(M_TILES):
+                    codes, plane = stationary(a, m)
+                    for b in range(2):
+                        cols = slice(h * PAIR + b * BANK, h * PAIR + (b + 1) * BANK)
+                        nc.tensor.matmul_mx(
+                            out=banks[m, b][:],
+                            lhsT=codes,
+                            lhsT_scale=plane,
+                            rhs=picked[a][:, cols].bitcast(E4M3),
+                            rhs_scale=picked_planes[PLANE[a] : P, cols],
+                            start=(a == 0),
+                            stop=(a == PASSES - 1),
+                        )
+            for m in range(M_TILES):
+                for b in range(2):
+                    cols = slice(b * BANK, (b + 1) * BANK)
+                    nc.vector.tensor_tensor(results[h, m][:, cols], banks[m, b][:], gates[h, m][:, cols], MULT)
+                nc.scalar.dma_start(out[m * P : (m + 1) * P, h * PAIR : (h + 1) * PAIR], results[h, m][:])

@@ -46,38 +46,48 @@ def tile_list_tabo_mul_kernel(tc, tab, w8, w4_words, w4_scales, gate, offs, out)
         w_plane = [keep.tile([P, N], U8, align_bytes=64, name=f"w_plane{a}") for a in range(W8_PASSES)]
         picked = [keep.tile([P, S], U32, align_bytes=64, name=f"picked{a}") for a in range(PASSES)]
         picked_planes = keep.tile([P, S], U8, align_bytes=64, name="picked_planes")
-        gates = {}
-        results = {}
-        for h in range(S // PAIR):
-            for m in range(M_TILES):
-                gates[h, m] = keep.tile([P, PAIR], F32, align_bytes=64, name=f"gate{h}{m}")
-                results[h, m] = keep.tile([P, PAIR], F32, align_bytes=64, name=f"result{h}{m}")
+        gates = [keep.tile([P, S], F32, align_bytes=64, name=f"gate{m}") for m in range(M_TILES)]
+        copies = [keep.tile([P, BANK], F32, align_bytes=64, name=f"copy{m}") for m in range(M_TILES)]
+        results = [keep.tile([P, S], F32, align_bytes=64, name=f"result{m}") for m in range(M_TILES)]
 
-        def load_words(a):
-            nc.sync.dma_start(words[a][:], tab[a, 0 : 512 * T].rearrange("(p b) -> p b", p=P).bitcast(I32))
+        def load_words(queue, a, lo, hi):
+            source = tab[a, 0 : 512 * T].rearrange("(p b) -> p b", p=P).bitcast(I32)
+            queue.dma_start(words[a][:, lo:hi], source[:, lo:hi])
 
-        load_words(0)
+        def load_w8(queue, a):
+            queue.dma_start(w_raw[a][:], w8[a * K_PASS : (a + 1) * K_PASS, :].rearrange("(p j) n -> p j n", j=PACK))
+
+        scale_rows = tab[:, 512 * T : 528 * T].rearrange("a (q t) -> a q t", q=16).bitcast(I32)
+
+        for half, queue in enumerate((nc.sync, nc.gpsimd)):
+            load_words(queue, 0, half * T // 2, (half + 1) * T // 2)
         nc.sync.dma_start(offsets[:], offs)
+        load_w8(nc.gpsimd, 0)
         nc.vector.memset(planes[:], 0)
         nc.vector.memset(w4_plane[:], 0)
+        nc.vector.memset(w4_codes[:, 0:32].bitcast(I32), 0)
+        nc.vector.memset(w_raw[1][:, 0, 0:8], 0.0)
+        for tile in words[1:]:
+            nc.vector.memset(tile[:, 0:8], 0)
+        for tile in gates:
+            nc.vector.memset(tile[:, 0:8], 0.0)
         for a in range(PASSES):
-            rows = tab[a, 512 * T : 528 * T].rearrange("(q t) -> q t", q=16).bitcast(I32)
             for quadrant in range(4):
                 first = 32 * quadrant + PLANE[a]
-                nc.gpsimd.dma_start(planes[first : first + ROWS, :], rows[ROWS * quadrant : ROWS * (quadrant + 1), :])
+                nc.sync.dma_start(
+                    planes[first : first + ROWS, :], scale_rows[a, ROWS * quadrant : ROWS * (quadrant + 1), :]
+                )
         for quadrant in range(4):
             nc.gpsimd.dma_start(
                 w4_plane[32 * quadrant : 32 * quadrant + ROWS, :],
                 w4_scales[0, ROWS * quadrant : ROWS * (quadrant + 1), :].bitcast(I32),
             )
-        for a in range(W8_PASSES):
-            nc.sync.dma_start(w_raw[a][:], w8[a * K_PASS : (a + 1) * K_PASS, :].rearrange("(p j) n -> p j n", j=PACK))
         nc.sync.dma_start(w4_codes[:].bitcast(I32), w4_words[0].bitcast(I32))
+        load_w8(nc.sync, 1)
         for a in range(1, PASSES):
-            load_words(a)
-        for h in range(S // PAIR):
-            for m in range(M_TILES):
-                nc.sync.dma_start(gates[h, m][:], gate[m * P : (m + 1) * P, h * PAIR : (h + 1) * PAIR])
+            load_words(nc.sync, a, 0, T)
+        for m in range(M_TILES):
+            nc.sync.dma_start(gates[m][:], gate[m * P : (m + 1) * P, :])
 
         def gather_words(a, lo, hi):
             nc.vector.tensor_copy(
@@ -94,36 +104,63 @@ def tile_list_tabo_mul_kernel(tc, tab, w8, w4_words, w4_scales, gate, offs, out)
                 in_=w_grouped[a][:].rearrange("p n j -> p (n j)"),
             )
         gather_words(1, 0, S)
-
         def stationary(a, m):
             cols = slice(m * P, (m + 1) * P)
             if a < W8_PASSES:
                 return w_codes[a][:, cols].bitcast(E4M3), w_plane[a][:, cols]
             return w4_codes[:, 2 * m * P : 2 * (m + 1) * P].bitcast(E2M1), w4_plane[:].bitcast(U8)[:, cols]
 
-        for h in range(S // PAIR):
-            for b in range(2):
-                gather_words(2, h * PAIR + b * BANK, h * PAIR + (b + 1) * BANK)
-            banks = {}
-            for m in range(M_TILES):
-                for b in range(2):
-                    banks[m, b] = psum.tile([P, BANK], F32, name=f"bank{m}{b}")
-            for a in range(PASSES):
-                for m in range(M_TILES):
-                    codes, plane = stationary(a, m)
-                    for b in range(2):
-                        cols = slice(h * PAIR + b * BANK, h * PAIR + (b + 1) * BANK)
-                        nc.tensor.matmul_mx(
-                            out=banks[m, b][:],
-                            lhsT=codes,
-                            lhsT_scale=plane,
-                            rhs=picked[a][:, cols].bitcast(E4M3),
-                            rhs_scale=picked_planes[PLANE[a] : P, cols],
-                            start=(a == 0),
-                            stop=(a == PASSES - 1),
-                        )
-            for m in range(M_TILES):
-                for b in range(2):
-                    cols = slice(b * BANK, (b + 1) * BANK)
-                    nc.vector.tensor_tensor(results[h, m][:, cols], banks[m, b][:], gates[h, m][:, cols], MULT)
-                nc.scalar.dma_start(out[m * P : (m + 1) * P, h * PAIR : (h + 1) * PAIR], results[h, m][:])
+        banks = {}
+
+        def multiply(a, m, b):
+            if a == 0:
+                banks[m, b] = psum.tile([P, BANK], F32, name=f"bank{m % 2}{b}")
+            codes, plane = stationary(a, m)
+            cols = slice(b * BANK, (b + 1) * BANK)
+            nc.tensor.matmul_mx(
+                out=banks[m, b][:],
+                lhsT=codes,
+                lhsT_scale=plane,
+                rhs=picked[a][:, cols].bitcast(E4M3),
+                rhs_scale=picked_planes[PLANE[a] : P, cols],
+                start=(a == 0),
+                stop=(a == PASSES - 1),
+            )
+
+        def finish(m, b):
+            cols = slice(b * BANK, (b + 1) * BANK)
+            if b == 0:
+                nc.scalar.activation(copies[m][:], banks[m, b][:], COPY)
+                nc.gpsimd.tensor_tensor(results[m][:, cols], copies[m][:], gates[m][:, cols], MULT)
+            else:
+                nc.vector.tensor_tensor(results[m][:, cols], banks[m, b][:], gates[m][:, cols], MULT)
+
+        def store(m, lo, hi):
+            nc.sync.dma_start(out[m * P : (m + 1) * P, lo:hi], results[m][:, lo:hi])
+
+        for a in range(W8_PASSES):
+            for m in range(2):
+                for b in range(S // BANK):
+                    multiply(a, m, b)
+        for half in range(2):
+            blocks = (2 * half, 2 * half + 1)
+            for b in blocks:
+                gather_words(2, b * BANK, (b + 1) * BANK)
+            for m in range(2):
+                for b in blocks:
+                    multiply(2, m, b)
+            for m in range(2):
+                for b in blocks:
+                    finish(m, b)
+                store(m, half * PAIR, (half + 1) * PAIR)
+        for m in range(2, M_TILES):
+            for b in range(S // BANK):
+                for a in range(PASSES):
+                    multiply(a, m, b)
+            for b in range(S // BANK):
+                finish(m, b)
+            if m == M_TILES - 1:
+                store(m, 0, PAIR)
+                store(m, PAIR, S)
+            else:
+                store(m, 0, S)

from contextlib import ExitStack

import concourse.mybir as mybir

O, K, N, T, S = 1024, 1536, 512, 4096, 2048
FLOPS = 2 * N * S * K

P = 128
PACK = 4
K_PASS = P * PACK
PASSES = K // K_PASS
W8_PASSES = O // K_PASS
M_TILES = N // P
BANK = 512
PAIR = 2 * BANK
ROWS = 4

F32 = mybir.dt.float32
BF16 = mybir.dt.bfloat16
I32 = mybir.dt.int32
U32 = mybir.dt.uint32
U16 = mybir.dt.uint16
U8 = mybir.dt.uint8
E4M3 = mybir.dt.float8_e4m3fn_x4
E2M1 = mybir.dt.float4_e2m1fn_x4
MULT = mybir.AluOpType.mult
COPY = mybir.ActivationFunctionType.Copy

PLANE = (4, 8, 0)


def tile_list_tabo_mul_kernel(tc, tab, w8, w4_words, w4_scales, gate, offs, out):
    nc = tc.nc
    with ExitStack() as ctx:
        keep = ctx.enter_context(tc.tile_pool(name="keep", bufs=1))
        psum = ctx.enter_context(tc.psum_pool(name="psum", bufs=1))

        offsets = keep.tile([P, S // 16], U16, name="offsets")
        words = [keep.tile([P, T], I32, align_bytes=64, name=f"words{a}") for a in range(PASSES)]
        planes = keep.tile([P, T // 4], I32, align_bytes=64, name="planes")
        w4_plane = keep.tile([P, N // 4], I32, align_bytes=64, name="w4_plane")
        w4_codes = keep.tile([P, 2 * N], U8, align_bytes=64, name="w4_codes")
        w_raw = [keep.tile([P, PACK, N], F32, align_bytes=64, name=f"w_raw{a}") for a in range(W8_PASSES)]
        w_grouped = [keep.tile([P, N, PACK], BF16, align_bytes=64, name=f"w_grouped{a}") for a in range(W8_PASSES)]
        w_codes = [keep.tile([P, N], U32, align_bytes=64, name=f"w_codes{a}") for a in range(W8_PASSES)]
        w_plane = [keep.tile([P, N], U8, align_bytes=64, name=f"w_plane{a}") for a in range(W8_PASSES)]
        picked = [keep.tile([P, S], U32, align_bytes=64, name=f"picked{a}") for a in range(PASSES)]
        picked_planes = keep.tile([P, S], U8, align_bytes=64, name="picked_planes")
        gates = [keep.tile([P, S], F32, align_bytes=64, name=f"gate{m}") for m in range(M_TILES)]
        copies = [keep.tile([P, BANK], F32, align_bytes=64, name=f"copy{m}") for m in range(M_TILES)]
        results = [keep.tile([P, S], F32, align_bytes=64, name=f"result{m}") for m in range(M_TILES)]

        def load_words(queue, a, lo, hi):
            source = tab[a, 0 : 512 * T].rearrange("(p b) -> p b", p=P).bitcast(I32)
            queue.dma_start(words[a][:, lo:hi], source[:, lo:hi])

        def load_w8(queue, a):
            queue.dma_start(w_raw[a][:], w8[a * K_PASS : (a + 1) * K_PASS, :].rearrange("(p j) n -> p j n", j=PACK))

        scale_rows = tab[:, 512 * T : 528 * T].rearrange("a (q t) -> a q t", q=16).bitcast(I32)

        for half, queue in enumerate((nc.sync, nc.gpsimd)):
            load_words(queue, 0, half * T // 2, (half + 1) * T // 2)
        nc.sync.dma_start(offsets[:], offs)
        load_w8(nc.gpsimd, 0)
        nc.vector.memset(planes[:], 0)
        nc.vector.memset(w4_plane[:], 0)
        nc.vector.memset(w4_codes[:, 0:32].bitcast(I32), 0)
        nc.vector.memset(w_raw[1][:, 0, 0:8], 0.0)
        for tile in words[1:]:
            nc.vector.memset(tile[:, 0:8], 0)
        for tile in gates:
            nc.vector.memset(tile[:, 0:8], 0.0)
        for a in range(PASSES):
            for quadrant in range(4):
                first = 32 * quadrant + PLANE[a]
                nc.sync.dma_start(
                    planes[first : first + ROWS, :], scale_rows[a, ROWS * quadrant : ROWS * (quadrant + 1), :]
                )
        for quadrant in range(4):
            nc.gpsimd.dma_start(
                w4_plane[32 * quadrant : 32 * quadrant + ROWS, :],
                w4_scales[0, ROWS * quadrant : ROWS * (quadrant + 1), :].bitcast(I32),
            )
        nc.sync.dma_start(w4_codes[:].bitcast(I32), w4_words[0].bitcast(I32))
        load_w8(nc.sync, 1)
        for a in range(1, PASSES):
            load_words(nc.sync, a, 0, T)
        for m in range(M_TILES):
            nc.sync.dma_start(gates[m][:], gate[m * P : (m + 1) * P, :])

        def gather_words(a, lo, hi):
            nc.vector.tensor_copy(
                picked[a][:, lo:hi], words[a][:].bitcast(U32).indirect(offsets[:, lo // 16 : hi // 16])
            )

        gather_words(0, 0, S)
        nc.vector.tensor_copy(picked_planes[:], planes[:].bitcast(U8).indirect(offsets[:]))
        for a in range(W8_PASSES):
            nc.scalar.activation(w_grouped[a][:], w_raw[a][:].rearrange("p j n -> p n j"), COPY)
            nc.vector.quantize_mx(
                out=w_codes[a][:].bitcast(E4M3),
                scales=w_plane[a][:],
                in_=w_grouped[a][:].rearrange("p n j -> p (n j)"),
            )
        gather_words(1, 0, S)
        def stationary(a, m):
            cols = slice(m * P, (m + 1) * P)
            if a < W8_PASSES:
                return w_codes[a][:, cols].bitcast(E4M3), w_plane[a][:, cols]
            return w4_codes[:, 2 * m * P : 2 * (m + 1) * P].bitcast(E2M1), w4_plane[:].bitcast(U8)[:, cols]

        banks = {}

        def multiply(a, m, b):
            if a == 0:
                banks[m, b] = psum.tile([P, BANK], F32, name=f"bank{m % 2}{b}")
            codes, plane = stationary(a, m)
            cols = slice(b * BANK, (b + 1) * BANK)
            nc.tensor.matmul_mx(
                out=banks[m, b][:],
                lhsT=codes,
                lhsT_scale=plane,
                rhs=picked[a][:, cols].bitcast(E4M3),
                rhs_scale=picked_planes[PLANE[a] : P, cols],
                start=(a == 0),
                stop=(a == PASSES - 1),
            )

        def finish(m, b):
            cols = slice(b * BANK, (b + 1) * BANK)
            if b == 0:
                nc.scalar.activation(copies[m][:], banks[m, b][:], COPY)
                nc.gpsimd.tensor_tensor(results[m][:, cols], copies[m][:], gates[m][:, cols], MULT)
            else:
                nc.vector.tensor_tensor(results[m][:, cols], banks[m, b][:], gates[m][:, cols], MULT)

        def store(m, lo, hi):
            nc.sync.dma_start(out[m * P : (m + 1) * P, lo:hi], results[m][:, lo:hi])

        for a in range(W8_PASSES):
            for m in range(2):
                for b in range(S // BANK):
                    multiply(a, m, b)
        for half in range(2):
            blocks = (2 * half, 2 * half + 1)
            for b in blocks:
                gather_words(2, b * BANK, (b + 1) * BANK)
            for m in range(2):
                for b in blocks:
                    multiply(2, m, b)
            for m in range(2):
                for b in blocks:
                    finish(m, b)
                store(m, half * PAIR, (half + 1) * PAIR)
        for m in range(2, M_TILES):
            for b in range(S // BANK):
                for a in range(PASSES):
                    multiply(a, m, b)
            for b in range(S // BANK):
                finish(m, b)
            if m == M_TILES - 1:
                store(m, 0, PAIR)
                store(m, PAIR, S)
            else:
                store(m, 0, S)
